import numpy as np, ml_dtypes
CORES = [3,5,19,21,35,37,51,53,67,69]
N = 10
import mx_ref
NC = 256
BF = ml_dtypes.bfloat16
def setup_inputs(rng):
    def f(*shape):
        return mx_ref.flush((rng.standard_normal(shape, dtype=np.float32) * np.exp2(rng.integers(-2, 3, shape[:-1] + (1,)))).astype(BF))
    return {"u": f(N, 128, 512), "v": f(N, 128, 512), "x": f(N, 128, 4 * NC)}
def setup_inputs_blocks(rng):
    d = setup_inputs(rng)
    for k in ("u", "v", "x"): d[k] = mx_ref.spread(d[k], rng, 4)
    return d
def setup_inputs_wide(rng):
    d = setup_inputs(rng)
    for k in ("u", "v", "x"): d[k] = mx_ref.flush((d[k].astype(np.float32) * np.exp2(rng.integers(-8, 9, (N, 1, 1))).astype(np.float32)).astype(BF))
    return d
def reference(u, v, x):
    QX = [mx_ref.quantize(x[j]) for j in range(N)]
    y = np.zeros((N, 128, N * NC), np.float32)
    for r in range(N):
        qu, qv = mx_ref.quantize(u[r]), mx_ref.quantize(v[r])
        for j in range(N):
            y[r][:, NC * j:NC * j + NC] = np.maximum(mx_ref.matmul(qu, QX[j]), np.float32(0)) * mx_ref.matmul(qv, QX[j])
    return {"y": y}

from concourse.bass import DstId, RemoteDMATransfer
from concourse.mybir import dt, AluOpType, ActivationFunctionType

NT = 10
W = 256
HALF = NT // 2
BANK = 512
NPAIR = 4

SCRATCH = {
    "xt": ("sbuf", [128, 4 * W], "bfloat16"),
    "ut": ("sbuf", [128, 512], "bfloat16"),
    "vt": ("sbuf", [128, 512], "bfloat16"),
    "qu": ("sbuf", [128, 128], "float8_e4m3fn_x4"),
    "su": ("sbuf", [128, 128], "uint8"),
    "qv": ("sbuf", [128, 128], "float8_e4m3fn_x4"),
    "sv": ("sbuf", [128, 128], "uint8"),
    "qx": ("sbuf", [128, NT * W], "float8_e4m3fn_x4"),
    "sx": ("sbuf", [128, NT * W], "uint8"),
    "ps": ("psum", [128, BANK * 2 * NPAIR], "float32"),
    "rl": ("sbuf", [128, NT * W], "float32"),
    "res": ("sbuf", [128, NT * W], "float32"),
}
SEMAPHORES = (["xl", "ul", "vl", "xq", "uq", "vq", "sent", "st", "psa", "pp0"]
              + ["%s%d" % (p, k) for p in ("ds", "dc", "pp") for k in range(1, HALF)]
              + ["%s%d" % (p, i) for p in ("mu", "mv", "re", "ml") for i in range(NT)])


def _bits(m):
    return bin(m).count("1")


def _split(mask, parts):
    es = [e for e in range(mask.bit_length()) if mask >> e & 1]
    per = len(es) // parts
    return [sum(1 << e for e in es[i * per:(i + 1) * per]) for i in range(parts)]


def _codes(T, a, b):
    return T.qx[:, W * a:W * b].bitcast(dt.uint8)


def _plane(T, a, b):
    return T.sx[:, W * a:W * b]


def rank_program(g, core, T, topo):
    if T.rank_of(core) is None:
        return
    S = T.sem
    cores = list(T.cores)
    chips = []
    for c in cores:
        if topo.chip(c) not in chips:
            chips.append(topo.chip(c))
    seat = {(topo.chip(c), topo.die(c)): c for c in cores}
    n = len(chips)
    my_chip, my_die = topo.chip(core), topo.die(core)
    ci = chips.index(my_chip)
    partner = [c for c in cores if topo.chip(c) == my_chip and c != core][0]
    far_die = topo.die(partner)
    to = [None] + [seat[(chips[(ci + k) % n], my_die)] for k in range(1, n)]
    tile_of = ([T.rank_of(seat[(chips[(ci - k) % n], my_die)]) for k in range(n)]
               + [T.rank_of(seat[(chips[(ci - k) % n], far_die)]) for k in range(n)])
    on = topo.mask(core, partner)
    off = on
    for k in range(1, n):
        off &= topo.mask(core, to[k])
    hi = on & ~off
    share = _split(off, n - 1)
    n_on, n_off, n_hi = _bits(on), _bits(off), _bits(hi)
    sent = [0]

    def call(items):
        trs = []
        for dst, out_ap, in_ap, sem, mask in items:
            if not topo.may_write(core, dst):
                raise ValueError("core %d may not write to core %d" % (core, dst))
            rid, pid, _ = topo.addr(dst)
            trs.append(RemoteDMATransfer(dst_ids=[DstId(rid=rid, pnc=pid)], dma_engine_mask=mask, remote_sem=sem,
                                         src=in_ap, dst=out_ap))
            sent[0] += _bits(mask)
        g.remote_dma_fused(trs, local_sem=S.sent)

    g.sync.dma_start(T.xt[0:64, :], T.x[0:64, :]).then_inc(S.xl, 16)
    g.scalar.dma_start(T.xt[64:128, :], T.x[64:128, :]).then_inc(S.xl, 16)
    g.sync.dma_start(T.ut[:], T.u[:]).then_inc(S.ul, 16)
    g.scalar.dma_start(T.vt[:], T.v[:]).then_inc(S.vl, 16)

    g.vector.wait_ge(S.xl, 32)
    g.vector.quantize_mx(T.qx[:, 0:W], T.sx[:, 0:W], T.xt[:]).then_inc(S.xq, 1)
    g.vector.wait_ge(S.ul, 16)
    g.vector.quantize_mx(T.qu[:], T.su[:], T.ut[:]).then_inc(S.uq, 1)
    g.vector.wait_ge(S.vl, 16)
    g.vector.quantize_mx(T.qv[:], T.sv[:], T.vt[:]).then_inc(S.vq, 1)

    g.wait_ge(S.xq, 1)
    call([(to[k], _plane(T, k, k + 1), _plane(T, 0, 1), S["ds%d" % k], share[k - 1]) for k in range(1, n)])
    call([(to[1], _codes(T, 1, 2), _codes(T, 0, 1), S.dc1, off),
          (partner, _codes(T, HALF, HALF + 1), _codes(T, 0, 1), S.pp0, hi)])
    call([(partner, _plane(T, HALF, HALF + 1), _plane(T, 0, 1), S.pp0, hi)])
    for k in range(2, n):
        call([(to[k], _codes(T, k, k + 1), _codes(T, 0, 1), S["dc%d" % k], off)])

    for k in range(1, n):
        g.wait_ge(S["ds%d" % k], _bits(share[k - 1]))
    call([(partner, _plane(T, HALF + 1, HALF + n), _plane(T, 1, n), S.psa, hi)])
    for k in range(1, n):
        g.wait_ge(S["dc%d" % k], n_off)
        call([(partner, _codes(T, HALF + k, HALF + k + 1), _codes(T, k, k + 1), S["pp%d" % k],
               on if k == n - 1 else hi)])
    g.wait_ge(S.sent, sent[0])

    def arrivals(s):
        if s == 0:
            return [(S.xq, 1), (S.uq, 1), (S.vq, 1)]
        if s < HALF:
            return [(S["ds%d" % s], _bits(share[s - 1])), (S["dc%d" % s], n_off)]
        if s == HALF:
            return [(S.pp0, 2 * n_hi)]
        k = s - HALF
        return [(S.psa, n_hi), (S["pp%d" % k], n_on if k == n - 1 else n_hi)]

    order = [0, HALF, 1, 2]
    for k in range(3, n):
        order += [k, HALF + k - 2]
    order += [HALF + n - 2, HALF + n - 1]

    done_at = {}
    for i, s in enumerate(order):
        col = W * tile_of[s]
        bu, bv = BANK * 2 * (i % NPAIR), BANK * (2 * (i % NPAIR) + 1)
        for sem, val in arrivals(s):
            g.tensor.wait_ge(sem, val)
        if i >= NPAIR:
            g.tensor.wait_ge(S["ml%d" % (i - NPAIR)], 1)
        rhs, rsc = T.qx[:, W * s:W * s + W], T.sx[:, W * s:W * s + W]
        g.tensor.matmul_mx(T.ps[:, bu:bu + W], T.qu[:], T.su[:], rhs, rsc, True, True).then_inc(S["mu%d" % i], 1)
        g.tensor.matmul_mx(T.ps[:, bv:bv + W], T.qv[:], T.sv[:], rhs, rsc, True, True).then_inc(S["mv%d" % i], 1)
        g.scalar.wait_ge(S["mu%d" % i], 1)
        g.scalar.activation(T.rl[:, W * i:W * i + W], T.ps[:, bu:bu + W], ActivationFunctionType.Relu).then_inc(
            S["re%d" % i], 1)
        g.vector.wait_ge(S["re%d" % i], 1)
        g.vector.wait_ge(S["mv%d" % i], 1)
        g.vector.tensor_tensor(T.res[:, col:col + W], T.rl[:, W * i:W * i + W], T.ps[:, bv:bv + W],
                               AluOpType.mult).then_inc(S["ml%d" % i], 1)
        done_at[s] = i

    stores = []
    for k in range(n):
        ia, ib = done_at[k], done_at[HALF + k]
        ca, cb = W * tile_of[k], W * tile_of[HALF + k]
        if k < n - 1 and abs(ca - cb) == W:
            stores.append((max(ia, ib), [ia, ib], min(ca, cb), min(ca, cb) + 2 * W))
        else:
            stores.append((ia, [ia], ca, ca + W))
            stores.append((ib, [ib], cb, cb + W))
    stores.sort()
    for _, idx, c0, c1 in stores:
        for i in idx:
            g.sync.wait_ge(S["ml%d" % i], 1)
        g.sync.dma_start(T.y[:, c0:c1], T.res[:, c0:c1]).then_inc(S.st, 16)
    g.sync.wait_ge(S.st, 16 * len(stores))
